import numpy as np
import ml_dtypes


def mxq(x, axis, fmt="e4m3"):
    dtype, down = {"e4m3": (ml_dtypes.float8_e4m3fn, 7), "e5m2": (ml_dtypes.float8_e5m2, 14)}[fmt]
    v = np.moveaxis(np.asarray(x, np.float32).astype(ml_dtypes.bfloat16).astype(np.float64), axis, -1)
    blocks = v.reshape(v.shape[:-1] + (-1, 32))
    amax = np.abs(blocks).max(-1, keepdims=True)
    byte = np.maximum(np.where(amax > 0, np.frexp(amax)[1] - 1 + 127, 0) - down, 1)
    scale = np.exp2(byte - 127.0)
    codes = (blocks / scale).astype(np.float32).astype(dtype).astype(np.float64)
    return np.moveaxis((codes * scale).reshape(v.shape), -1, axis)


WIDE = False


def mx_kscale(k):
    if not WIDE:
        return np.ones(k)
    levels = np.array([10, -10, 5, -5, 0])
    if k % 512:
        return np.exp2(np.random.permutation(np.resize(levels, k // 32))).repeat(32)
    a = np.empty((k // 512, 16))
    for p in range(k // 512):
        a[p, :8] = np.random.permutation(np.resize(levels, 8))
        for g in range(8):
            far = levels[np.abs(levels - a[p, g]) >= 10]
            a[p, g + 8] = far[np.random.randint(len(far))]
    return np.exp2(a.ravel()).repeat(32)


def f64(x):
    return np.asarray(x).astype(np.float64)


def striped(idx):
    return np.tile(idx.reshape(-1, 16).T, (8, 1)).astype(np.uint16)


def unstriped(offs):
    return offs[:16].T.reshape(-1).astype(np.int64)


E2M1 = np.array([0.0, 0.5, 1.0, 1.5, 2.0, 3.0, 4.0, 6.0, -0.0, -0.5, -1.0, -1.5, -2.0, -3.0, -4.0, -6.0])


def pack_weight(w, fmt):
    k, n = w.shape
    w = f64(np.asarray(w, np.float32).astype(ml_dtypes.bfloat16)).reshape(k // 32, 32, n)
    amax = np.abs(w).max(1)
    if fmt == "e4m3":
        byte = np.frexp(amax)[1] - 1 + 127 - 7
    else:
        mant, ex = np.frexp(amax / 6.0)
        byte = np.where(mant > 0.5, ex, ex - 1) + 127
    byte = np.clip(np.where(amax > 0, byte, 1), 1, 254)
    scaled = (w * np.exp2(127.0 - byte)[:, None, :]).reshape(k, n).astype(np.float32)
    by_word = np.ascontiguousarray(scaled.reshape(k // 512, 128, 4, n).transpose(0, 1, 3, 2))
    if fmt == "e4m3":
        words = by_word.astype(ml_dtypes.float8_e4m3fn).view(np.uint8)
    else:
        c = by_word.astype(ml_dtypes.float4_e2m1fn).view(np.uint8) & 0xF
        words = (c[..., 0::2] | (c[..., 1::2] << 4)).reshape(k // 512, 128, 2 * n)
    return np.ascontiguousarray(words), np.ascontiguousarray(byte.astype(np.uint8).reshape(k // 512, 16, n))


def unpack_weight(words, scales, fmt):
    g, _, n = scales.shape
    words = np.ascontiguousarray(words).reshape(g, 128, n, -1)
    if fmt == "e4m3":
        vals = words.view(ml_dtypes.float8_e4m3fn).astype(np.float64)
    else:
        nib = np.empty((g, 128, n, 4), np.uint8)
        nib[..., 0::2] = words & 0xF
        nib[..., 1::2] = words >> 4
        vals = E2M1[nib]
    vals = vals * np.repeat(np.exp2(scales.astype(np.float64) - 127.0), 8, axis=1)[..., None]
    return vals.transpose(0, 1, 3, 2).reshape(g * 512, n)


def gelu(v):
    return 0.5 * v * (1.0 + np.tanh(np.sqrt(2.0 / np.pi) * (v + 0.044715 * v**3)))


K, T, E, C, N = 1024, 640, 2, 256, 128
K8 = 512


def by_expert(wq, xq):
    return np.concatenate([wq[e].T @ xq[:, e * C:(e + 1) * C] for e in range(E)], axis=1)


def setup_inputs():
    n = np.random.standard_normal
    s = mx_kscale(K)[:, None]
    w = n((E, K, N)) / np.sqrt(K) / s[None]
    w8 = [pack_weight(m[:K8], "e4m3") for m in w]
    w4 = [pack_weight(m[K8:], "e2m1") for m in w]
    return {
        "xT": (n((K, T)) * s).astype(np.float32),
        "w8_words": np.stack([m[0] for m in w8]),
        "w8_scales": np.stack([m[1] for m in w8]),
        "w4_words": np.stack([m[0] for m in w4]),
        "w4_scales": np.stack([m[1] for m in w4]),
        "b": (0.3 * n((N, E))).astype(np.float32),
        "gate": np.tile(np.random.uniform(0.2, 1.0, E * C), (N, 1)).astype(np.float32),
        "offs": striped(np.random.permutation(T)[:E * C]),
        "dst": striped(np.random.permutation(T)[:E * C]),
    }


def reference(xT, w8_words, w8_scales, w4_words, w4_scales, b, gate, offs, dst):
    idx = unstriped(offs)
    w = np.stack([np.concatenate([unpack_weight(w8_words[e], w8_scales[e], "e4m3"), unpack_weight(w4_words[e], w4_scales[e], "e2m1")]) for e in range(E)])
    xq = mxq(f64(xT)[:, idx], 0, "e4m3")
    y = by_expert(w, xq)
    y = gelu(y + np.repeat(f64(b), C, axis=1))
    out = np.zeros((N, T))
    out[:, unstriped(dst)] = f64(gate) * y
    return out

@@ -1,0 +1,119 @@
+import concourse.mybir as mybir
+
+E, K, N, T, C = 2, 1024, 128, 640, 256
+FLOPS = 2 * K * N * E * C
+
+F32 = mybir.dt.float32
+BF16 = mybir.dt.bfloat16
+I32 = mybir.dt.int32
+U32 = mybir.dt.uint32
+U16 = mybir.dt.uint16
+U8 = mybir.dt.uint8
+FP8X4 = mybir.dt.float8_e4m3fn_x4
+FP4X4 = mybir.dt.float4_e2m1fn_x4
+ACT = mybir.ActivationFunctionType
+MULT = mybir.AluOpType.mult
+
+P = 128
+CHUNKS = {
+    0: [(0, 256, 128), (256, 640, 152)],
+    1: [(0, 384, 152), (384, 640, 168)],
+}
+QUANT = {0: [(0, 256), (256, 512), (512, 640)], 1: [(0, 256), (256, 384), (384, 640)]}
+PLANE = [4, 0]
+
+
+def tile_moe_two_lin_gelu_kernel(
+    tc, xT, w8_words, w8_scales, w4_words, w4_scales, b, gate, offs, dst, out
+):
+    nc = tc.nc
+    with (
+        tc.tile_pool(name="keep", bufs=1) as keep,
+        tc.psum_pool(name="psum", bufs=1) as psum,
+    ):
+        offs_t = keep.tile([P, E * C // 16], U16, name="offs_t")
+        dst_t = keep.tile([P, E * C // 16], U16, name="dst_t")
+        x_t = [[keep.tile([P, 4, e - s], F32, name=f"x{a}{i}", align_bytes=64) for i, (s, e, v) in enumerate(CHUNKS[a])] for a in range(2)]
+        xb = [keep.tile([P, T, 4], BF16, name=f"xb{a}", align_bytes=64) for a in range(2)]
+        words = [keep.tile([P, T], U32, name=f"words{a}", align_bytes=64) for a in range(2)]
+        plane = keep.tile([P, T], U8, name="plane", align_bytes=64)
+        gwords = [keep.tile([P, E * C], U32, name=f"gwords{a}", align_bytes=64) for a in range(2)]
+        gplane = keep.tile([P, E * C], U8, name="gplane", align_bytes=64)
+        w8 = keep.tile([P, E, 4 * N], U8, name="w8", align_bytes=64)
+        w4 = keep.tile([P, E, 2 * N], U8, name="w4", align_bytes=64)
+        ws = keep.tile([P, 2, E, N], U8, name="ws", align_bytes=64)
+        b_t = keep.tile([P, E], F32, name="b_t")
+        gate_t = keep.tile([P, E * C], F32, name="gate_t")
+        y = [keep.tile([P, C], F32, name=f"y{e}") for e in range(E)]
+        out_t = keep.tile([P, T], F32, name="out_t")
+        warm = keep.tile([P, 1], F32, name="warm")
+        acc = [[psum.tile([P, 512], F32, name=f"acc{e}{h}") for h in range(2)] for e in range(E)]
+
+        xv = [xT[512 * a : 512 * (a + 1), :].rearrange("(p j) t -> p j t", j=4) for a in range(2)]
+        for a in range(2):
+            for i, (s, e, v) in enumerate(CHUNKS[a]):
+                nc.sync.dma_start(out=x_t[a][i][:], in_=xv[a][:, :, s:e])
+            if a == 0:
+                nc.sync.dma_start(out=offs_t[:], in_=offs)
+        nc.vector.memset(ws[:].rearrange("p f e n -> p (f e n)").bitcast(I32), 0)
+        nc.vector.memset(warm[:], 0.0)
+        nc.vector.memset(plane[:].bitcast(I32), 0)
+        nc.vector.memset(out_t[:], 0.0)
+        for f, (src, queue) in enumerate(((w8_scales, nc.scalar), (w4_scales, nc.gpsimd))):
+            for q in range(4):
+                queue.dma_start(
+                    out=ws[32 * q : 32 * q + 4, f, :, :].bitcast(I32),
+                    in_=src[:, 0, 4 * q : 4 * q + 4, :].rearrange("e q n -> q e n").bitcast(I32),
+                )
+        nc.gpsimd.dma_start(out=b_t[:], in_=b)
+        nc.scalar.activation(warm[:], warm[:], ACT.Gelu_apprx_tanh)
+        nc.sync.dma_start(out=w8[:].bitcast(I32), in_=w8_words.rearrange("e a p n r -> p (e a) (n r)").bitcast(I32))
+        nc.sync.dma_start(out=w4[:].bitcast(I32), in_=w4_words.rearrange("e a p n -> p (e a) n").bitcast(I32))
+        nc.sync.dma_start(out=gate_t[:], in_=gate)
+        nc.sync.dma_start(out=dst_t[:], in_=dst)
+
+        def cast(a, i):
+            s, e, v = CHUNKS[a][i]
+            nc.scalar.copy(xb[a][:, s + v : e, :], x_t[a][i][:, :, v:].rearrange("p j t -> p t j"))
+            nc.vector.tensor_copy(xb[a][:, s : s + v, :], x_t[a][i][:, :, :v].rearrange("p j t -> p t j"))
+
+        def quant(a, s, e):
+            nc.vector.quantize_mx(
+                out=words[a][:, s:e].bitcast(FP8X4),
+                scales=plane[PLANE[a] :, s:e],
+                in_=xb[a][:, s:e, :].rearrange("p t j -> p (t j)"),
+            )
+
+        def lists(t, e):
+            return t[:, 16 * e : 16 * (e + 1)]
+
+        def gather(out_tile, table, e):
+            nc.vector.tensor_copy(out_tile[:, C * e : C * (e + 1)], table[:].indirect(lists(offs_t, e)))
+
+        cast(0, 0)
+        quant(0, *QUANT[0][0])
+        cast(0, 1)
+        quant(0, *QUANT[0][1])
+        quant(0, *QUANT[0][2])
+        for e in range(E):
+            gather(gwords[0], words[0], e)
+        cast(1, 0)
+        quant(1, *QUANT[1][0])
+        quant(1, *QUANT[1][1])
+        cast(1, 1)
+        quant(1, *QUANT[1][2])
+        for e in range(E):
+            gather(gplane, plane, e)
+            gather(gwords[1], words[1], e)
+            halves = [slice(C * e + 128 * h, C * e + 128 * (h + 1)) for h in range(2)]
+            for a, w in enumerate((w8[:, e, :].bitcast(FP8X4), w4[:, e, :].bitcast(FP4X4))):
+                for h, cols in enumerate(halves):
+                    nc.tensor.matmul_mx(
+                        out=acc[e][h][:, :128], lhsT=w, lhsT_scale=ws[:, a, e, :],
+                        rhs=gwords[a][:, cols].bitcast(FP8X4), rhs_scale=gplane[PLANE[a] :, cols], start=(a == 0), stop=(a == 1),
+                    )
+            for h in range(2):
+                nc.scalar.activation(y[e][:, 128 * h : 128 * (h + 1)], acc[e][h][:, :128], ACT.Gelu_apprx_tanh, bias=b_t[:, e : e + 1])
+        for e in range(E):
+            nc.vector.tensor_tensor(out_t[:].indirect(lists(dst_t, e)), y[e][:], gate_t[:, C * e : C * (e + 1)], MULT)
+        nc.sync.dma_start(out=out, in_=out_t[:])

@@ -16,10 +16,9 @@ MULT = mybir.AluOpType.mult
 
 P = 128
 CHUNKS = {
-    0: [(0, 256, 128), (256, 640, 152)],
-    1: [(0, 384, 152), (384, 640, 168)],
+    0: [(0, 256), (256, 640)],
+    1: [(0, 384), (384, 640)],
 }
-QUANT = {0: [(0, 256), (256, 512), (512, 640)], 1: [(0, 256), (256, 384), (384, 640)]}
 PLANE = [4, 0]
 
 
@@ -33,7 +32,7 @@ def tile_moe_two_lin_gelu_kernel(
     ):
         offs_t = keep.tile([P, E * C // 16], U16, name="offs_t")
         dst_t = keep.tile([P, E * C // 16], U16, name="dst_t")
-        x_t = [[keep.tile([P, 4, e - s], F32, name=f"x{a}{i}", align_bytes=64) for i, (s, e, v) in enumerate(CHUNKS[a])] for a in range(2)]
+        x_t = [[keep.tile([P, 4, e - s], F32, name=f"x{a}{i}", align_bytes=64) for i, (s, e) in enumerate(CHUNKS[a])] for a in range(2)]
         xb = [keep.tile([P, T, 4], BF16, name=f"xb{a}", align_bytes=64) for a in range(2)]
         words = [keep.tile([P, T], U32, name=f"words{a}", align_bytes=64) for a in range(2)]
         plane = keep.tile([P, T], U8, name="plane", align_bytes=64)
@@ -51,7 +50,7 @@ def tile_moe_two_lin_gelu_kernel(
 
         xv = [xT[512 * a : 512 * (a + 1), :].rearrange("(p j) t -> p j t", j=4) for a in range(2)]
         for a in range(2):
-            for i, (s, e, v) in enumerate(CHUNKS[a]):
+            for i, (s, e) in enumerate(CHUNKS[a]):
                 nc.sync.dma_start(out=x_t[a][i][:], in_=xv[a][:, :, s:e])
             if a == 0:
                 nc.sync.dma_start(out=offs_t[:], in_=offs)
@@ -72,10 +71,14 @@ def tile_moe_two_lin_gelu_kernel(
         nc.sync.dma_start(out=gate_t[:], in_=gate)
         nc.sync.dma_start(out=dst_t[:], in_=dst)
 
-        def cast(a, i):
-            s, e, v = CHUNKS[a][i]
-            nc.scalar.copy(xb[a][:, s + v : e, :], x_t[a][i][:, :, v:].rearrange("p j t -> p t j"))
-            nc.vector.tensor_copy(xb[a][:, s : s + v, :], x_t[a][i][:, :, :v].rearrange("p j t -> p t j"))
+        def cast(engine, a, s, e):
+            i = 0 if e <= CHUNKS[a][0][1] else 1
+            c0 = CHUNKS[a][i][0]
+            copy = nc.scalar.copy if engine == "S" else nc.vector.tensor_copy
+            copy(
+                xb[a][:, s:e, :].rearrange("p (c i) j -> p c j i", i=4),
+                x_t[a][i][:, :, s - c0 : e - c0].rearrange("p j (c i) -> p c j i", i=4),
+            )
 
         def quant(a, s, e):
             nc.vector.quantize_mx(
@@ -90,18 +93,20 @@ def tile_moe_two_lin_gelu_kernel(
         def gather(out_tile, table, e):
             nc.vector.tensor_copy(out_tile[:, C * e : C * (e + 1)], table[:].indirect(lists(offs_t, e)))
 
-        cast(0, 0)
-        quant(0, *QUANT[0][0])
-        cast(0, 1)
-        quant(0, *QUANT[0][1])
-        quant(0, *QUANT[0][2])
+        cast("S", 0, 0, 256)
+        quant(0, 0, 256)
+        cast("S", 0, 256, 384)
+        cast("V", 0, 384, 640)
+        quant(0, 256, 512)
+        quant(0, 512, 640)
+        cast("S", 1, 0, 256)
+        cast("S", 1, 256, 384)
         for e in range(E):
             gather(gwords[0], words[0], e)
-        cast(1, 0)
-        quant(1, *QUANT[1][0])
-        quant(1, *QUANT[1][1])
-        cast(1, 1)
-        quant(1, *QUANT[1][2])
+        quant(1, 0, 256)
+        cast("V", 1, 384, 640)
+        quant(1, 256, 384)
+        quant(1, 384, 640)
         for e in range(E):
             gather(gplane, plane, e)
             gather(gwords[1], words[1], e)

@@ -16,7 +16,7 @@ MULT = mybir.AluOpType.mult
 
 P = 128
 CHUNKS = {
-    0: [(0, 256), (256, 640)],
+    0: [(0, 384), (384, 640)],
     1: [(0, 384), (384, 640)],
 }
 PLANE = [4, 0]
@@ -93,18 +93,20 @@ def tile_moe_two_lin_gelu_kernel(
         def gather(out_tile, table, e):
             nc.vector.tensor_copy(out_tile[:, C * e : C * (e + 1)], table[:].indirect(lists(offs_t, e)))
 
-        cast("S", 0, 0, 256)
+        cast("S", 0, 0, 192)
+        cast("V", 0, 192, 384)
         quant(0, 0, 256)
-        cast("S", 0, 256, 384)
-        cast("V", 0, 384, 640)
-        quant(0, 256, 512)
-        quant(0, 512, 640)
+        quant(0, 256, 384)
+        cast("S", 0, 544, 640)
+        cast("V", 0, 384, 544)
+        quant(0, 384, 640)
         cast("S", 1, 0, 256)
-        cast("S", 1, 256, 384)
         for e in range(E):
             gather(gwords[0], words[0], e)
+        cast("V", 1, 256, 384)
+        cast("S", 1, 544, 640)
+        cast("V", 1, 384, 544)
         quant(1, 0, 256)
-        cast("V", 1, 384, 640)
         quant(1, 256, 384)
         quant(1, 384, 640)
         for e in range(E):

import concourse.mybir as mybir

E, K, N, T, C = 2, 1024, 128, 640, 256
FLOPS = 2 * K * N * E * C

F32 = mybir.dt.float32
BF16 = mybir.dt.bfloat16
I32 = mybir.dt.int32
U32 = mybir.dt.uint32
U16 = mybir.dt.uint16
U8 = mybir.dt.uint8
FP8X4 = mybir.dt.float8_e4m3fn_x4
FP4X4 = mybir.dt.float4_e2m1fn_x4
ACT = mybir.ActivationFunctionType
MULT = mybir.AluOpType.mult

P = 128
CHUNKS = {
    0: [(0, 384), (384, 640)],
    1: [(0, 384), (384, 640)],
}
PLANE = [4, 0]


def tile_moe_two_lin_gelu_kernel(
    tc, xT, w8_words, w8_scales, w4_words, w4_scales, b, gate, offs, dst, out
):
    nc = tc.nc
    with (
        tc.tile_pool(name="keep", bufs=1) as keep,
        tc.psum_pool(name="psum", bufs=1) as psum,
    ):
        offs_t = keep.tile([P, E * C // 16], U16, name="offs_t")
        dst_t = keep.tile([P, E * C // 16], U16, name="dst_t")
        x_t = [[keep.tile([P, 4, e - s], F32, name=f"x{a}{i}", align_bytes=64) for i, (s, e) in enumerate(CHUNKS[a])] for a in range(2)]
        xb = [keep.tile([P, T, 4], BF16, name=f"xb{a}", align_bytes=64) for a in range(2)]
        words = [keep.tile([P, T], U32, name=f"words{a}", align_bytes=64) for a in range(2)]
        plane = keep.tile([P, T], U8, name="plane", align_bytes=64)
        gwords = [keep.tile([P, E * C], U32, name=f"gwords{a}", align_bytes=64) for a in range(2)]
        gplane = keep.tile([P, E * C], U8, name="gplane", align_bytes=64)
        w8 = keep.tile([P, E, 4 * N], U8, name="w8", align_bytes=64)
        w4 = keep.tile([P, E, 2 * N], U8, name="w4", align_bytes=64)
        ws = keep.tile([P, 2, E, N], U8, name="ws", align_bytes=64)
        b_t = keep.tile([P, E], F32, name="b_t")
        gate_t = keep.tile([P, E * C], F32, name="gate_t")
        y = [keep.tile([P, C], F32, name=f"y{e}") for e in range(E)]
        out_t = keep.tile([P, T], F32, name="out_t")
        warm = keep.tile([P, 1], F32, name="warm")
        acc = [[psum.tile([P, 512], F32, name=f"acc{e}{h}") for h in range(2)] for e in range(E)]

        xv = [xT[512 * a : 512 * (a + 1), :].rearrange("(p j) t -> p j t", j=4) for a in range(2)]
        for a in range(2):
            for i, (s, e) in enumerate(CHUNKS[a]):
                nc.sync.dma_start(out=x_t[a][i][:], in_=xv[a][:, :, s:e])
            if a == 0:
                nc.sync.dma_start(out=offs_t[:], in_=offs)
        nc.vector.memset(ws[:].rearrange("p f e n -> p (f e n)").bitcast(I32), 0)
        nc.vector.memset(warm[:], 0.0)
        nc.vector.memset(plane[:].bitcast(I32), 0)
        nc.vector.memset(out_t[:], 0.0)
        for f, (src, queue) in enumerate(((w8_scales, nc.scalar), (w4_scales, nc.gpsimd))):
            for q in range(4):
                queue.dma_start(
                    out=ws[32 * q : 32 * q + 4, f, :, :].bitcast(I32),
                    in_=src[:, 0, 4 * q : 4 * q + 4, :].rearrange("e q n -> q e n").bitcast(I32),
                )
        nc.gpsimd.dma_start(out=b_t[:], in_=b)
        nc.scalar.activation(warm[:], warm[:], ACT.Gelu_apprx_tanh)
        nc.sync.dma_start(out=w8[:].bitcast(I32), in_=w8_words.rearrange("e a p n r -> p (e a) (n r)").bitcast(I32))
        nc.sync.dma_start(out=w4[:].bitcast(I32), in_=w4_words.rearrange("e a p n -> p (e a) n").bitcast(I32))
        nc.sync.dma_start(out=gate_t[:], in_=gate)
        nc.sync.dma_start(out=dst_t[:], in_=dst)

        def cast(engine, a, s, e):
            i = 0 if e <= CHUNKS[a][0][1] else 1
            c0 = CHUNKS[a][i][0]
            copy = nc.scalar.copy if engine == "S" else nc.vector.tensor_copy
            copy(
                xb[a][:, s:e, :].rearrange("p (c i) j -> p c j i", i=4),
                x_t[a][i][:, :, s - c0 : e - c0].rearrange("p j (c i) -> p c j i", i=4),
            )

        def quant(a, s, e):
            nc.vector.quantize_mx(
                out=words[a][:, s:e].bitcast(FP8X4),
                scales=plane[PLANE[a] :, s:e],
                in_=xb[a][:, s:e, :].rearrange("p t j -> p (t j)"),
            )

        def lists(t, e):
            return t[:, 16 * e : 16 * (e + 1)]

        def gather(out_tile, table, e):
            nc.vector.tensor_copy(out_tile[:, C * e : C * (e + 1)], table[:].indirect(lists(offs_t, e)))

        cast("S", 0, 0, 192)
        cast("V", 0, 192, 384)
        quant(0, 0, 256)
        quant(0, 256, 384)
        cast("S", 0, 544, 640)
        cast("V", 0, 384, 544)
        quant(0, 384, 640)
        cast("S", 1, 0, 256)
        for e in range(E):
            gather(gwords[0], words[0], e)
        cast("V", 1, 256, 384)
        cast("S", 1, 544, 640)
        cast("V", 1, 384, 544)
        quant(1, 0, 256)
        quant(1, 256, 384)
        quant(1, 384, 640)
        for e in range(E):
            gather(gplane, plane, e)
            gather(gwords[1], words[1], e)
            halves = [slice(C * e + 128 * h, C * e + 128 * (h + 1)) for h in range(2)]
            for a, w in enumerate((w8[:, e, :].bitcast(FP8X4), w4[:, e, :].bitcast(FP4X4))):
                for h, cols in enumerate(halves):
                    nc.tensor.matmul_mx(
                        out=acc[e][h][:, :128], lhsT=w, lhsT_scale=ws[:, a, e, :],
                        rhs=gwords[a][:, cols].bitcast(FP8X4), rhs_scale=gplane[PLANE[a] :, cols], start=(a == 0), stop=(a == 1),
                    )
            for h in range(2):
                nc.scalar.activation(y[e][:, 128 * h : 128 * (h + 1)], acc[e][h][:, :128], ACT.Gelu_apprx_tanh, bias=b_t[:, e : e + 1])
        for e in range(E):
            nc.vector.tensor_tensor(out_t[:].indirect(lists(dst_t, e)), y[e][:], gate_t[:, C * e : C * (e + 1)], MULT)
        nc.sync.dma_start(out=out, in_=out_t[:])
